import numpy as np
import ml_dtypes


def mxq(x, axis, fmt="e4m3"):
    dtype, down = {"e4m3": (ml_dtypes.float8_e4m3fn, 7), "e5m2": (ml_dtypes.float8_e5m2, 14)}[fmt]
    v = np.moveaxis(np.asarray(x, np.float32).astype(ml_dtypes.bfloat16).astype(np.float64), axis, -1)
    blocks = v.reshape(v.shape[:-1] + (-1, 32))
    amax = np.abs(blocks).max(-1, keepdims=True)
    byte = np.maximum(np.where(amax > 0, np.frexp(amax)[1] - 1 + 127, 0) - down, 1)
    scale = np.exp2(byte - 127.0)
    codes = (blocks / scale).astype(np.float32).astype(dtype).astype(np.float64)
    return np.moveaxis((codes * scale).reshape(v.shape), -1, axis)


WIDE = False


def mx_kscale(k):
    if not WIDE:
        return np.ones(k)
    levels = np.array([10, -10, 5, -5, 0])
    if k % 512:
        return np.exp2(np.random.permutation(np.resize(levels, k // 32))).repeat(32)
    a = np.empty((k // 512, 16))
    for p in range(k // 512):
        a[p, :8] = np.random.permutation(np.resize(levels, 8))
        for g in range(8):
            far = levels[np.abs(levels - a[p, g]) >= 10]
            a[p, g + 8] = far[np.random.randint(len(far))]
    return np.exp2(a.ravel()).repeat(32)


def f64(x):
    return np.asarray(x).astype(np.float64)


def striped(idx):
    return np.tile(idx.reshape(-1, 16).T, (8, 1)).astype(np.uint16)


def unstriped(offs):
    return offs[:16].T.reshape(-1).astype(np.int64)


def sigmoid(v):
    return 1.0 / (1.0 + np.exp(-np.maximum(v, -700.0)))


K, T, D, S, V, N = 512, 4096, 2, 1536, 768, 256


def setup_inputs():
    n = np.random.standard_normal
    s = mx_kscale(K)[:, None]
    return {
        "xT": (n((K, T)) * s).astype(np.float32),
        "w": (n((D, K, N)) / np.sqrt(K) / s[None]).astype(np.float32),
        "b": (0.3 * n((N, 1))).astype(np.float32),
        "offs": striped(np.random.permutation(T)[:S]),
    }


def reference(xT, w, b, offs):
    idx = unstriped(offs)
    xq = mxq(f64(xT)[:, idx], 0, "e4m3")
    wq = mxq(f64(w), 1, "e4m3")
    y0 = wq[0].T @ xq[:, :V]
    y1 = wq[1].T @ xq[:, V:]
    return y0 * sigmoid(y1 + f64(b))

@@ -1,0 +1,124 @@
+from contextlib import ExitStack
+
+import concourse.mybir as mybir
+
+K, T, S, V, N = 512, 4096, 1536, 768, 256
+FLOPS = 2 * K * N * S
+
+F32 = mybir.dt.float32
+BF16 = mybir.dt.bfloat16
+U16 = mybir.dt.uint16
+U32 = mybir.dt.uint32
+U8 = mybir.dt.uint8
+FP8X4 = mybir.dt.float8_e4m3fn_x4
+MULT, ADD = mybir.AluOpType.mult, mybir.AluOpType.add
+SIGMOID = mybir.ActivationFunctionType.Sigmoid
+
+P = 128
+J = 4
+C = 512
+M = 128
+
+
+def tile_picked_pair_lin_gate_sub_e_kernel(tc, xT, w, b, offs, out):
+    nc = tc.nc
+    x_rows = xT.rearrange("(p j) t -> p j t", j=J)
+
+    with ExitStack() as ctx:
+        keep = ctx.enter_context(tc.tile_pool(name="keep", bufs=1))
+        psum = ctx.enter_context(tc.psum_pool(name="psum", bufs=1))
+
+        list_sb = keep.tile([P, S // 16], U16, name="list_sb")
+        planes = [keep.tile([P, T], F32, name=f"plane{j}") for j in range(J)]
+        w_raw = [keep.tile([P, J, N], F32, name=f"w_raw{d}") for d in range(2)]
+        bias = [keep.tile([P, 1], F32, name=f"bias{m}") for m in range(2)]
+        nc.sync.dma_start(list_sb[:], offs)
+        for j in range(J):
+            nc.sync.dma_start(planes[j][:], x_rows[:, j, :])
+        for d in (1, 0):
+            nc.sync.dma_start(w_raw[d][:], w[d].rearrange("(p j) n -> p j n", j=J))
+        for m in range(2):
+            nc.sync.dma_start(bias[m][:], b[m * M : (m + 1) * M, :])
+
+        warm = keep.tile([P, 1], F32, name="warm")
+        warm_out = keep.tile([P, 1], F32, name="warm_out")
+        nc.vector.memset(warm[:], 0.0)
+        nc.scalar.activation(warm_out[:], warm[:], SIGMOID)
+
+        starts = {"z": 0, "y": C, "x": 2 * C}
+
+        def picks(s):
+            return list_sb[:, starts[s] // 16 : (starts[s] + C) // 16]
+
+        early = {s: keep.tile([P, 2, C], F32, name=f"early_{s}") for s in "zyx"}
+        late = keep.tile([P, 2, C], F32, name="late")
+        grouped = {s: keep.tile([P, C, J], BF16, name=f"grouped_{s}", align_bytes=64) for s in "zyx"}
+        codes = {s: keep.tile([P, C], U32, name=f"codes_{s}", align_bytes=64) for s in "zyx"}
+        scales = {s: keep.tile([P, C], U8, name=f"scales_{s}", align_bytes=64) for s in "zyx"}
+
+        for j in range(2):
+            for s in "zyx":
+                nc.vector.tensor_copy(early[s][:, j, :], planes[j][:].indirect(picks(s)))
+        for s in "zyx":
+            nc.scalar.copy(grouped[s][:, :, 0:2], early[s][:].rearrange("p u n -> p n u"))
+        for s in "yz":
+            nc.vector.tensor_copy(grouped[s][:, :, 2], planes[2][:].indirect(picks(s)))
+        nc.vector.tensor_copy(late[:, 0, :], planes[2][:].indirect(picks("x")))
+        nc.vector.tensor_copy(late[:, 1, :], planes[3][:].indirect(picks("x")))
+        nc.scalar.copy(grouped["x"][:, :, 2:4], late[:].rearrange("p u n -> p n u"))
+        nc.vector.tensor_copy(grouped["y"][:, :, 3], planes[3][:].indirect(picks("y")))
+
+        w_grouped = [keep.tile([P, N, J], BF16, name=f"w_grouped{d}", align_bytes=64) for d in range(2)]
+        w_codes = [keep.tile([P, N], U32, name=f"w_codes{d}", align_bytes=64) for d in range(2)]
+        w_scales = [keep.tile([P, N], U8, name=f"w_scales{d}", align_bytes=64) for d in range(2)]
+        for d in (1, 0):
+            nc.gpsimd.tensor_scalar(w_grouped[d][:], w_raw[d][:].rearrange("p j n -> p n j"), 1.0, 0.0, MULT, ADD)
+
+        def quantize(codes_t, scales_t, grouped_t):
+            nc.vector.quantize_mx(
+                out=codes_t[:].bitcast(FP8X4), scales=scales_t[:], in_=grouped_t[:].rearrange("p n j -> p (n j)")
+            )
+
+        def multiply(acc, d, m, s, c0, c1):
+            cols = slice(m * M, (m + 1) * M)
+            nc.tensor.matmul_mx(
+                out=acc,
+                lhsT=w_codes[d][:, cols].bitcast(FP8X4),
+                lhsT_scale=w_scales[d][:, cols],
+                rhs=codes[s][:, c0:c1].bitcast(FP8X4),
+                rhs_scale=scales[s][:, c0:c1],
+                start=True,
+                stop=True,
+            )
+
+        gate = [keep.tile([P, V], F32, name=f"gate{m}") for m in range(2)]
+        result = [keep.tile([P, V], F32, name=f"result{m}") for m in range(2)]
+        HALF = C // 2
+
+        quantize(w_codes[1], w_scales[1], w_grouped[1])
+        quantize(codes["x"], scales["x"], grouped["x"])
+        for m in range(2):
+            acc = psum.tile([P, C], F32, name=f"y1x{m}")
+            multiply(acc[:], 1, m, "x", 0, C)
+            nc.scalar.activation(gate[m][:, HALF:V], acc[:], SIGMOID, bias=bias[m][:])
+        quantize(codes["y"], scales["y"], grouped["y"])
+        quantize(w_codes[0], w_scales[0], w_grouped[0])
+        accs = []
+        for m in range(2):
+            acc = psum.tile([P, HALF], F32, name=f"y1y{m}")
+            multiply(acc[:], 1, m, "y", HALF, C)
+            nc.scalar.activation(gate[m][:, 0:HALF], acc[:], SIGMOID, bias=bias[m][:])
+        for m in range(2):
+            acc = psum.tile([P, HALF], F32, name=f"y0y{m}")
+            multiply(acc[:], 0, m, "y", 0, HALF)
+            accs.append(acc)
+        nc.vector.tensor_copy(grouped["z"][:, :, 3], planes[3][:].indirect(picks("z")))
+        quantize(codes["z"], scales["z"], grouped["z"])
+        for m in range(2):
+            acc = psum.tile([P, C], F32, name=f"y0z{m}")
+            multiply(acc[:], 0, m, "z", 0, C)
+            accs.append(acc)
+        for i, cols in ((0, slice(C, V)), (1, slice(C, V)), (2, slice(0, C)), (3, slice(0, C))):
+            m = i % 2
+            nc.vector.tensor_tensor(result[m][:, cols], accs[i][:], gate[m][:, cols], MULT)
+            nc.sync.dma_start(out[m * M : (m + 1) * M, cols], result[m][:, cols])

@@ -51,8 +51,8 @@ def tile_picked_pair_lin_gate_sub_e_kernel(tc, xT, w, b, offs, out):
             return list_sb[:, starts[s] // 16 : (starts[s] + C) // 16]
 
         early = {s: keep.tile([P, 2, C], F32, name=f"early_{s}") for s in "zyx"}
-        late = keep.tile([P, 2, C], F32, name="late")
-        grouped = {s: keep.tile([P, C, J], BF16, name=f"grouped_{s}", align_bytes=64) for s in "zyx"}
+        late = {s: keep.tile([P, 2, C], F32, name=f"late_{s}") for s in "yx"}
+        grouped = {s: keep.tile([P, C, J], BF16, name=f"grouped_{s}", tag=f"turn_{s}", align_bytes=64) for s in "zyx"}
         codes = {s: keep.tile([P, C], U32, name=f"codes_{s}", align_bytes=64) for s in "zyx"}
         scales = {s: keep.tile([P, C], U8, name=f"scales_{s}", align_bytes=64) for s in "zyx"}
 
@@ -61,22 +61,22 @@ def tile_picked_pair_lin_gate_sub_e_kernel(tc, xT, w, b, offs, out):
                 nc.vector.tensor_copy(early[s][:, j, :], planes[j][:].indirect(picks(s)))
         for s in "zyx":
             nc.scalar.copy(grouped[s][:, :, 0:2], early[s][:].rearrange("p u n -> p n u"))
-        for s in "yz":
-            nc.vector.tensor_copy(grouped[s][:, :, 2], planes[2][:].indirect(picks(s)))
-        nc.vector.tensor_copy(late[:, 0, :], planes[2][:].indirect(picks("x")))
-        nc.vector.tensor_copy(late[:, 1, :], planes[3][:].indirect(picks("x")))
-        nc.scalar.copy(grouped["x"][:, :, 2:4], late[:].rearrange("p u n -> p n u"))
-        nc.vector.tensor_copy(grouped["y"][:, :, 3], planes[3][:].indirect(picks("y")))
+        for j in range(2, J):
+            for s in "xy":
+                nc.vector.tensor_copy(late[s][:, j - 2, :], planes[j][:].indirect(picks(s)))
+            nc.vector.tensor_copy(grouped["z"][:, :, j], planes[j][:].indirect(picks("z")))
 
         w_grouped = [keep.tile([P, N, J], BF16, name=f"w_grouped{d}", align_bytes=64) for d in range(2)]
-        w_codes = [keep.tile([P, N], U32, name=f"w_codes{d}", align_bytes=64) for d in range(2)]
+        w_codes = {}
         w_scales = [keep.tile([P, N], U8, name=f"w_scales{d}", align_bytes=64) for d in range(2)]
         for d in (1, 0):
             nc.gpsimd.tensor_scalar(w_grouped[d][:], w_raw[d][:].rearrange("p j n -> p n j"), 1.0, 0.0, MULT, ADD)
 
-        def quantize(codes_t, scales_t, grouped_t):
+        def quantize(codes_t, scales_t, grouped_t, c0, c1):
             nc.vector.quantize_mx(
-                out=codes_t[:].bitcast(FP8X4), scales=scales_t[:], in_=grouped_t[:].rearrange("p n j -> p (n j)")
+                out=codes_t[:, c0:c1].bitcast(FP8X4),
+                scales=scales_t[:, c0:c1],
+                in_=grouped_t[:].rearrange("p n j -> p (n j)")[:, J * c0 : J * c1],
             )
 
         def multiply(acc, d, m, s, c0, c1):
@@ -95,30 +95,40 @@ def tile_picked_pair_lin_gate_sub_e_kernel(tc, xT, w, b, offs, out):
         result = [keep.tile([P, V], F32, name=f"result{m}") for m in range(2)]
         HALF = C // 2
 
-        quantize(w_codes[1], w_scales[1], w_grouped[1])
-        quantize(codes["x"], scales["x"], grouped["x"])
+        for s in "xy":
+            nc.scalar.copy(grouped[s][:, :, 2:4], late[s][:].rearrange("p u n -> p n u"))
+
+        quantize(codes["x"], scales["x"], grouped["x"], 0, C)
+        w_codes[1] = keep.tile([P, N], U32, name="w_codes1", tag="turn_x", align_bytes=64)
+        quantize(w_codes[1], w_scales[1], w_grouped[1], 0, N)
         for m in range(2):
             acc = psum.tile([P, C], F32, name=f"y1x{m}")
             multiply(acc[:], 1, m, "x", 0, C)
             nc.scalar.activation(gate[m][:, HALF:V], acc[:], SIGMOID, bias=bias[m][:])
-        quantize(codes["y"], scales["y"], grouped["y"])
-        quantize(w_codes[0], w_scales[0], w_grouped[0])
-        accs = []
+        quantize(codes["y"], scales["y"], grouped["y"], 0, C)
+        w_codes[0] = keep.tile([P, N], U32, name="w_codes0", tag="turn_y", align_bytes=64)
+        quantize(w_codes[0], w_scales[0], w_grouped[0], 0, N)
+        y0y = [psum.tile([P, HALF], F32, name=f"y0y{m}") for m in range(2)]
+        for m in range(2):
+            multiply(y0y[m][:], 0, m, "y", 0, HALF)
         for m in range(2):
             acc = psum.tile([P, HALF], F32, name=f"y1y{m}")
             multiply(acc[:], 1, m, "y", HALF, C)
             nc.scalar.activation(gate[m][:, 0:HALF], acc[:], SIGMOID, bias=bias[m][:])
-        for m in range(2):
-            acc = psum.tile([P, HALF], F32, name=f"y0y{m}")
-            multiply(acc[:], 0, m, "y", 0, HALF)
-            accs.append(acc)
-        nc.vector.tensor_copy(grouped["z"][:, :, 3], planes[3][:].indirect(picks("z")))
-        quantize(codes["z"], scales["z"], grouped["z"])
-        for m in range(2):
-            acc = psum.tile([P, C], F32, name=f"y0z{m}")
-            multiply(acc[:], 0, m, "z", 0, C)
-            accs.append(acc)
-        for i, cols in ((0, slice(C, V)), (1, slice(C, V)), (2, slice(0, C)), (3, slice(0, C))):
-            m = i % 2
-            nc.vector.tensor_tensor(result[m][:, cols], accs[i][:], gate[m][:, cols], MULT)
+        y0z = [psum.tile([P, C], F32, name=f"y0z{m}") for m in range(2)]
+        for h in (1, 0):
+            c0, c1 = h * HALF, (h + 1) * HALF
+            quantize(codes["z"], scales["z"], grouped["z"], c0, c1)
+            for m in range(2):
+                multiply(y0z[m][:, c0:c1], 0, m, "z", c0, c1)
+
+        def finish(acc, m, c0):
+            cols = slice(c0, c0 + HALF)
+            nc.vector.tensor_tensor(result[m][:, cols], acc, gate[m][:, cols], MULT)
             nc.sync.dma_start(out[m * M : (m + 1) * M, cols], result[m][:, cols])
+
+        for m in range(2):
+            finish(y0y[m][:], m, C)
+        for h in (1, 0):
+            for m in range(2):
+                finish(y0z[m][:, h * HALF : (h + 1) * HALF], m, h * HALF)

from contextlib import ExitStack

import concourse.mybir as mybir

K, T, S, V, N = 512, 4096, 1536, 768, 256
FLOPS = 2 * K * N * S

F32 = mybir.dt.float32
BF16 = mybir.dt.bfloat16
U16 = mybir.dt.uint16
U32 = mybir.dt.uint32
U8 = mybir.dt.uint8
FP8X4 = mybir.dt.float8_e4m3fn_x4
MULT, ADD = mybir.AluOpType.mult, mybir.AluOpType.add
SIGMOID = mybir.ActivationFunctionType.Sigmoid

P = 128
J = 4
C = 512
M = 128


def tile_picked_pair_lin_gate_sub_e_kernel(tc, xT, w, b, offs, out):
    nc = tc.nc
    x_rows = xT.rearrange("(p j) t -> p j t", j=J)

    with ExitStack() as ctx:
        keep = ctx.enter_context(tc.tile_pool(name="keep", bufs=1))
        psum = ctx.enter_context(tc.psum_pool(name="psum", bufs=1))

        list_sb = keep.tile([P, S // 16], U16, name="list_sb")
        planes = [keep.tile([P, T], F32, name=f"plane{j}") for j in range(J)]
        w_raw = [keep.tile([P, J, N], F32, name=f"w_raw{d}") for d in range(2)]
        bias = [keep.tile([P, 1], F32, name=f"bias{m}") for m in range(2)]
        nc.sync.dma_start(list_sb[:], offs)
        for j in range(J):
            nc.sync.dma_start(planes[j][:], x_rows[:, j, :])
        for d in (1, 0):
            nc.sync.dma_start(w_raw[d][:], w[d].rearrange("(p j) n -> p j n", j=J))
        for m in range(2):
            nc.sync.dma_start(bias[m][:], b[m * M : (m + 1) * M, :])

        warm = keep.tile([P, 1], F32, name="warm")
        warm_out = keep.tile([P, 1], F32, name="warm_out")
        nc.vector.memset(warm[:], 0.0)
        nc.scalar.activation(warm_out[:], warm[:], SIGMOID)

        starts = {"z": 0, "y": C, "x": 2 * C}

        def picks(s):
            return list_sb[:, starts[s] // 16 : (starts[s] + C) // 16]

        early = {s: keep.tile([P, 2, C], F32, name=f"early_{s}") for s in "zyx"}
        late = {s: keep.tile([P, 2, C], F32, name=f"late_{s}") for s in "yx"}
        grouped = {s: keep.tile([P, C, J], BF16, name=f"grouped_{s}", tag=f"turn_{s}", align_bytes=64) for s in "zyx"}
        codes = {s: keep.tile([P, C], U32, name=f"codes_{s}", align_bytes=64) for s in "zyx"}
        scales = {s: keep.tile([P, C], U8, name=f"scales_{s}", align_bytes=64) for s in "zyx"}

        for j in range(2):
            for s in "zyx":
                nc.vector.tensor_copy(early[s][:, j, :], planes[j][:].indirect(picks(s)))
        for s in "zyx":
            nc.scalar.copy(grouped[s][:, :, 0:2], early[s][:].rearrange("p u n -> p n u"))
        for j in range(2, J):
            for s in "xy":
                nc.vector.tensor_copy(late[s][:, j - 2, :], planes[j][:].indirect(picks(s)))
            nc.vector.tensor_copy(grouped["z"][:, :, j], planes[j][:].indirect(picks("z")))

        w_grouped = [keep.tile([P, N, J], BF16, name=f"w_grouped{d}", align_bytes=64) for d in range(2)]
        w_codes = {}
        w_scales = [keep.tile([P, N], U8, name=f"w_scales{d}", align_bytes=64) for d in range(2)]
        for d in (1, 0):
            nc.gpsimd.tensor_scalar(w_grouped[d][:], w_raw[d][:].rearrange("p j n -> p n j"), 1.0, 0.0, MULT, ADD)

        def quantize(codes_t, scales_t, grouped_t, c0, c1):
            nc.vector.quantize_mx(
                out=codes_t[:, c0:c1].bitcast(FP8X4),
                scales=scales_t[:, c0:c1],
                in_=grouped_t[:].rearrange("p n j -> p (n j)")[:, J * c0 : J * c1],
            )

        def multiply(acc, d, m, s, c0, c1):
            cols = slice(m * M, (m + 1) * M)
            nc.tensor.matmul_mx(
                out=acc,
                lhsT=w_codes[d][:, cols].bitcast(FP8X4),
                lhsT_scale=w_scales[d][:, cols],
                rhs=codes[s][:, c0:c1].bitcast(FP8X4),
                rhs_scale=scales[s][:, c0:c1],
                start=True,
                stop=True,
            )

        gate = [keep.tile([P, V], F32, name=f"gate{m}") for m in range(2)]
        result = [keep.tile([P, V], F32, name=f"result{m}") for m in range(2)]
        HALF = C // 2

        for s in "xy":
            nc.scalar.copy(grouped[s][:, :, 2:4], late[s][:].rearrange("p u n -> p n u"))

        quantize(codes["x"], scales["x"], grouped["x"], 0, C)
        w_codes[1] = keep.tile([P, N], U32, name="w_codes1", tag="turn_x", align_bytes=64)
        quantize(w_codes[1], w_scales[1], w_grouped[1], 0, N)
        for m in range(2):
            acc = psum.tile([P, C], F32, name=f"y1x{m}")
            multiply(acc[:], 1, m, "x", 0, C)
            nc.scalar.activation(gate[m][:, HALF:V], acc[:], SIGMOID, bias=bias[m][:])
        quantize(codes["y"], scales["y"], grouped["y"], 0, C)
        w_codes[0] = keep.tile([P, N], U32, name="w_codes0", tag="turn_y", align_bytes=64)
        quantize(w_codes[0], w_scales[0], w_grouped[0], 0, N)
        y0y = [psum.tile([P, HALF], F32, name=f"y0y{m}") for m in range(2)]
        for m in range(2):
            multiply(y0y[m][:], 0, m, "y", 0, HALF)
        for m in range(2):
            acc = psum.tile([P, HALF], F32, name=f"y1y{m}")
            multiply(acc[:], 1, m, "y", HALF, C)
            nc.scalar.activation(gate[m][:, 0:HALF], acc[:], SIGMOID, bias=bias[m][:])
        y0z = [psum.tile([P, C], F32, name=f"y0z{m}") for m in range(2)]
        for h in (1, 0):
            c0, c1 = h * HALF, (h + 1) * HALF
            quantize(codes["z"], scales["z"], grouped["z"], c0, c1)
            for m in range(2):
                multiply(y0z[m][:, c0:c1], 0, m, "z", c0, c1)

        def finish(acc, m, c0):
            cols = slice(c0, c0 + HALF)
            nc.vector.tensor_tensor(result[m][:, cols], acc, gate[m][:, cols], MULT)
            nc.sync.dma_start(out[m * M : (m + 1) * M, cols], result[m][:, cols])

        for m in range(2):
            finish(y0y[m][:], m, C)
        for h in (1, 0):
            for m in range(2):
                finish(y0z[m][:, h * HALF : (h + 1) * HALF], m, h * HALF)
